import numpy as np
import ml_dtypes


def mxq(x, axis, fmt="e4m3"):
    dtype, down = {"e4m3": (ml_dtypes.float8_e4m3fn, 7), "e5m2": (ml_dtypes.float8_e5m2, 14)}[fmt]
    v = np.moveaxis(np.asarray(x, np.float32).astype(ml_dtypes.bfloat16).astype(np.float64), axis, -1)
    blocks = v.reshape(v.shape[:-1] + (-1, 32))
    amax = np.abs(blocks).max(-1, keepdims=True)
    byte = np.maximum(np.where(amax > 0, np.frexp(amax)[1] - 1 + 127, 0) - down, 1)
    scale = np.exp2(byte - 127.0)
    codes = (blocks / scale).astype(np.float32).astype(dtype).astype(np.float64)
    return np.moveaxis((codes * scale).reshape(v.shape), -1, axis)


WIDE = False


def mx_kscale(k):
    if not WIDE:
        return np.ones(k)
    levels = np.array([10, -10, 5, -5, 0])
    if k % 512:
        return np.exp2(np.random.permutation(np.resize(levels, k // 32))).repeat(32)
    a = np.empty((k // 512, 16))
    for p in range(k // 512):
        a[p, :8] = np.random.permutation(np.resize(levels, 8))
        for g in range(8):
            far = levels[np.abs(levels - a[p, g]) >= 10]
            a[p, g + 8] = far[np.random.randint(len(far))]
    return np.exp2(a.ravel()).repeat(32)


BF16 = ml_dtypes.bfloat16


def bf(x):
    return np.asarray(x, np.float32).astype(BF16)


def f64(x):
    return np.asarray(x).astype(np.float64)


E2M1 = np.array([0.0, 0.5, 1.0, 1.5, 2.0, 3.0, 4.0, 6.0, -0.0, -0.5, -1.0, -1.5, -2.0, -3.0, -4.0, -6.0])


def pack_weight(w, fmt):
    k, n = w.shape
    w = f64(bf(w)).reshape(k // 32, 32, n)
    amax = np.abs(w).max(1)
    if fmt == "e4m3":
        byte = np.frexp(amax)[1] - 1 + 127 - 7
    else:
        mant, ex = np.frexp(amax / 6.0)
        byte = np.where(mant > 0.5, ex, ex - 1) + 127
    byte = np.clip(np.where(amax > 0, byte, 1), 1, 254)
    scaled = (w * np.exp2(127.0 - byte)[:, None, :]).reshape(k, n).astype(np.float32)
    by_word = np.ascontiguousarray(scaled.reshape(k // 512, 128, 4, n).transpose(0, 1, 3, 2))
    if fmt == "e4m3":
        words = by_word.astype(ml_dtypes.float8_e4m3fn).view(np.uint8)
    else:
        c = by_word.astype(ml_dtypes.float4_e2m1fn).view(np.uint8) & 0xF
        words = c[..., 0::2] | (c[..., 1::2] << 4)
    return np.ascontiguousarray(words), np.ascontiguousarray(byte.astype(np.uint8).reshape(k // 512, 16, n))


def unpack_weight(words, scales, fmt):
    g, p, n, _ = words.shape
    if fmt == "e4m3":
        vals = np.ascontiguousarray(words).view(ml_dtypes.float8_e4m3fn).astype(np.float64)
    else:
        nib = np.empty((g, p, n, 4), np.uint8)
        nib[..., 0::2] = words & 0xF
        nib[..., 1::2] = words >> 4
        vals = E2M1[nib]
    vals = vals * np.repeat(np.exp2(scales.astype(np.float64) - 127.0), 8, axis=1)[..., None]
    return vals.transpose(0, 1, 3, 2).reshape(g * 512, n)
def pack4(w):
    words, scales = pack_weight(w, "e2m1")
    return words.reshape(words.shape[0], 128, -1), scales


def unpack4(words, scales):
    return unpack_weight(words.reshape(words.shape[0], 128, -1, 2), scales, "e2m1")


MH, ML, N, R = 1024, 3072, 2048, 512


def setup_inputs():
    s = mx_kscale(MH)
    t = mx_kscale(ML)
    y_heavy = 1.5 * np.random.standard_normal((MH, R))
    y_rest = 1.5 * np.random.standard_normal((ML, R))
    d_heavy = (1 + 0.1 * np.random.standard_normal(MH)) * s
    d_rest = (1 + 0.1 * np.random.standard_normal(ML)) * t
    c = 1 + 0.1 * np.random.standard_normal(N)
    a_heavy = np.random.standard_normal((MH, N)) / np.sqrt(MH) / s[:, None]
    a_rest = np.random.standard_normal((ML, N)) / np.sqrt(ML) / t[:, None]
    rest_words, rest_scales = pack4(a_rest)
    return {"y_heavy": bf(y_heavy), "y_rest": bf(y_rest),
            "d_heavy": bf(d_heavy), "d_rest": bf(d_rest), "c": bf(c),
            "a_heavy": bf(a_heavy),
            "rest_words": rest_words, "rest_scales": rest_scales}


def reference(y_heavy, y_rest, d_heavy, d_rest, c, a_heavy, rest_words, rest_scales):
    sh = np.tanh(f64(y_heavy)) * f64(d_heavy)[:, None]
    sl = np.tanh(f64(y_rest)) * f64(d_rest)[:, None]
    zh = mxq(f64(a_heavy), 0, "e4m3").T @ mxq(sh, 0, "e4m3")
    zl = unpack4(rest_words, rest_scales).T @ mxq(sl, 0, "e4m3")
    return (zh + zl) * f64(c)[:, None]

@@ -1,0 +1,310 @@
+from contextlib import ExitStack
+
+import concourse.mybir as mybir
+from concourse.masks import make_identity
+
+F32 = mybir.dt.float32
+BF16 = mybir.dt.bfloat16
+I32 = mybir.dt.int32
+U32 = mybir.dt.uint32
+U8 = mybir.dt.uint8
+FP8X4 = mybir.dt.float8_e4m3fn_x4
+FP4X4 = mybir.dt.float4_e2m1fn_x4
+ACT = mybir.ActivationFunctionType
+ALU = mybir.AluOpType
+
+MH, ML, N, R = 1024, 3072, 2048, 512
+FLOPS = 2 * (MH + ML) * N * R
+
+P = 128
+PACK = 4
+K_PASS = P * PACK
+REST = ML // K_PASS
+PASSES = (MH + ML) // K_PASS
+N_TILES = N // P
+HALF = N // 2
+FIRST = 4
+PAIR = 2
+
+
+def tile_hager_adjoint_step_s1_kernel(
+    tc, y_heavy, y_rest, d_heavy, d_rest, c, a_heavy, rest_words, rest_scales, out
+):
+    nc = tc.nc
+
+    with ExitStack() as ctx:
+        keep = ctx.enter_context(tc.tile_pool(name="keep", bufs=1))
+        stream = ctx.enter_context(tc.tile_pool(name="stream", bufs=4))
+        banks = ctx.enter_context(tc.psum_pool(name="banks", bufs=1))
+        ctx.enter_context(tc.manual_schedule())
+
+        warm = keep.tile([P, 1], F32, name="warm")
+        nc.gpsimd.memset(warm[:], 0.0)
+        ident = keep.tile([P, P], BF16, name="ident")
+        make_identity(nc, ident[:])
+        rows = keep.tile([P, K_PASS + P], BF16, name="rows", align_bytes=64)
+        nc.vector.memset(rows[:], 0.0)
+
+        def plane(name, groups):
+            t = keep.tile([P, groups, HALF], U8, name=name, align_bytes=64)
+            nc.vector.memset(t[:].rearrange("p g n -> p (g n)").bitcast(I32), 0)
+            return t
+
+        scales_lo_first = plane("scales_lo_first", FIRST)
+        scales_lo_later = plane("scales_lo_later", REST - FIRST)
+        scales_hi = plane("scales_hi", REST)
+
+        nc.scalar.dma_start(out=rows[0:4, :K_PASS], in_=d_rest[0 : 4 * K_PASS].rearrange("(g k) -> g k", k=K_PASS))
+        nc.scalar.dma_start(out=rows[4:6, :K_PASS], in_=d_rest[4 * K_PASS : ML].rearrange("(g k) -> g k", k=K_PASS))
+        nc.scalar.dma_start(out=rows[6:8, :K_PASS], in_=d_heavy.rearrange("(g k) -> g k", k=K_PASS))
+        nc.scalar.dma_start(out=rows[0:N_TILES, K_PASS:], in_=c.rearrange("(n m) -> n m", m=P))
+        nc.scalar.activation(out=warm[:], in_=warm[:], func=ACT.Tanh)
+
+        y_tiles = {}
+
+        def load_y(g, cols):
+            src = y_rest if g < REST else y_heavy
+            row0 = (g if g < REST else g - REST) * K_PASS
+            width = cols.stop - cols.start
+            t = keep.tile([P, PACK, width], BF16, name="y" + str(g) + "_" + str(cols.start))
+            nc.sync.dma_start(out=t[:], in_=src[row0 : row0 + K_PASS, cols].rearrange("(p j) w -> p j w", j=PACK))
+            for q0 in range(cols.start, cols.stop, P):
+                y_tiles[g, q0] = (t, q0 - cols.start)
+
+        words = {}
+
+        def load_words(g0, g1, half):
+            t = keep.tile([P, g1 - g0, 2 * HALF], U8, name="w" + str(half) + "_" + str(g0), align_bytes=64)
+            src = rest_words[g0:g1, :, half * 2 * HALF : (half + 1) * 2 * HALF].rearrange("g p b -> p g b")
+            nc.sync.dma_start(out=t[:].bitcast(I32), in_=src.bitcast(I32))
+            for g in range(g0, g1):
+                words[g, half] = t[:, g - g0, :]
+
+        planes = {}
+
+        def load_scales(t, g0, g1, half):
+            src = rest_scales[g0:g1, :, half * HALF : (half + 1) * HALF].rearrange("g q n -> q g n")
+            for quad in range(4):
+                nc.sync.dma_start(
+                    out=t[32 * quad : 32 * quad + 4, :, :].bitcast(I32),
+                    in_=src[4 * quad : 4 * quad + 4, :, :].bitcast(I32),
+                )
+            for g in range(g0, g1):
+                planes[g, half] = t[:, g - g0, :]
+
+        a_tiles = {}
+
+        def load_a(g, half):
+            row0 = (g - REST) * K_PASS
+            t = keep.tile([P, PACK, HALF], BF16, name="a" + str(g) + "_" + str(half))
+            src = a_heavy[row0 : row0 + K_PASS, half * HALF : (half + 1) * HALF]
+            nc.sync.dma_start(out=t[:], in_=src.rearrange("(p j) n -> p j n", j=PACK))
+            a_tiles[g, half] = t
+
+        whole = slice(0, R)
+        load_y(0, slice(0, R // 2))
+        load_y(0, slice(R // 2, R))
+        load_y(1, whole)
+        load_words(0, 1, 0)
+        load_scales(scales_lo_first, 0, FIRST, 0)
+        load_words(1, 2, 0)
+        load_y(2, whole)
+        load_words(2, FIRST, 0)
+        load_y(3, whole)
+        load_words(0, FIRST, 1)
+        load_y(4, whole)
+        load_scales(scales_hi, 0, REST, 1)
+        load_words(FIRST, REST, 1)
+        for g in range(5, PASSES):
+            load_y(g, whole)
+        for g in range(REST, PASSES):
+            load_a(g, 1)
+        load_scales(scales_lo_later, FIRST, REST, 0)
+        load_words(FIRST, REST, 0)
+        for g in range(REST, PASSES):
+            load_a(g, 0)
+
+        turned = banks.tile([P, PACK + 1, P], BF16, name="turned", tag="bank7")
+        for j in range(PACK):
+            nc.tensor.transpose(turned[:, j, :], rows[:, j:K_PASS:PACK], ident[:])
+        nc.tensor.transpose(turned[:, PACK, :], rows[:, K_PASS:], ident[:])
+        d_cols = keep.tile([P, PASSES, PACK], F32, name="d_cols")
+        nc.vector.tensor_copy(out=d_cols[:], in_=turned[:, :PACK, :PASSES].rearrange("p j g -> p g j"))
+        c_cols = keep.tile([P, N_TILES], F32, name="c_cols")
+        nc.vector.tensor_copy(out=c_cols[:], in_=turned[:, PACK, :N_TILES])
+
+        s_codes = [keep.tile([P, R], U32, name="s_codes" + str(g), align_bytes=64) for g in range(PASSES)]
+        s_scales = [keep.tile([P, R], U8, name="s_scales" + str(g), align_bytes=64) for g in range(PASSES)]
+        smooth = {}
+        scaled = {}
+
+        def tanh(piece):
+            g, r0, r1 = piece
+            y, at = y_tiles[g, r0]
+            t = stream.tile([P, r1 - r0, PACK], F32, name="smooth", tag="smooth", bufs=4)
+            nc.scalar.activation(
+                out=t[:], in_=y[:, :, at : at + r1 - r0].rearrange("p j w -> p w j"), func=ACT.Tanh
+            )
+            smooth[piece] = t
+
+        def scale_rows(piece):
+            g, r0, r1 = piece
+            t = stream.tile([P, r1 - r0, PACK], BF16, name="scaled", tag="scaled", bufs=4, align_bytes=64)
+            d = d_cols[:, g, :].unsqueeze(1).to_broadcast([P, r1 - r0, PACK])
+            nc.vector.tensor_tensor(out=t[:], in0=smooth[piece][:], in1=d, op=ALU.mult)
+            scaled[piece] = t
+
+        def quantize_s(piece):
+            g, r0, r1 = piece
+            nc.vector.quantize_mx(
+                out=s_codes[g][:, r0:r1].bitcast(FP8X4),
+                scales=s_scales[g][:, r0:r1],
+                in_=scaled[piece][:].rearrange("p w j -> p (w j)"),
+            )
+
+        grouped = {}
+        a_codes = {}
+        a_scales = {}
+
+        def group_a(g, n0, engine):
+            t = stream.tile([P, PAIR * P, PACK], BF16, name="grouped", tag="grouped", bufs=8, align_bytes=64)
+            at = n0 * P % HALF
+            src = a_tiles[g, n0 * P // HALF][:, :, at : at + PAIR * P]
+            src = src.rearrange("p j n -> p n j")
+            dst = t[:]
+            if engine == "scalar":
+                nc.scalar.copy(out=dst, in_=src)
+            else:
+                nc.vector.tensor_copy(out=dst, in_=src)
+            grouped[g, n0] = t
+
+        def quantize_a(g, n0):
+            codes = keep.tile([P, PAIR * P], U32, name="a_codes" + str(g) + "_" + str(n0), align_bytes=64)
+            scales = keep.tile([P, PAIR * P], U8, name="a_scales" + str(g) + "_" + str(n0), align_bytes=64)
+            nc.vector.quantize_mx(
+                out=codes[:].bitcast(FP8X4), scales=scales[:], in_=grouped[g, n0][:].rearrange("p n j -> p (n j)")
+            )
+            for i in range(PAIR):
+                a_codes[g, n0 + i] = codes[:, i * P : (i + 1) * P]
+                a_scales[g, n0 + i] = scales[:, i * P : (i + 1) * P]
+
+        sums = {}
+
+        def open_sum(n):
+            sums[n] = banks.tile([P, R], F32, name="sum" + str(n % 8), tag="bank" + str(n % 8))
+
+        def multiply(n, g, start, stop):
+            if g < REST:
+                half, at = divmod(n, N_TILES // 2)
+                codes = words[g, half][:, 2 * P * at : 2 * P * (at + 1)].bitcast(FP4X4)
+                scales = planes[g, half][:, P * at : P * (at + 1)]
+            else:
+                codes = a_codes[g, n].bitcast(FP8X4)
+                scales = a_scales[g, n]
+            nc.tensor.matmul_mx(
+                out=sums[n][:],
+                lhsT=codes,
+                lhsT_scale=scales,
+                rhs=s_codes[g][:].bitcast(FP8X4),
+                rhs_scale=s_scales[g][:],
+                start=start,
+                stop=stop,
+            )
+
+        parked = {}
+
+        def park(n, engine):
+            t = keep.tile([P, R], F32, name="parked" + str(n))
+            if engine == "scalar":
+                nc.scalar.activation(out=t[:], in_=sums[n][:], func=ACT.Copy, scale=c_cols[:, n : n + 1])
+            else:
+                nc.vector.tensor_scalar(
+                    out=t[:], in0=sums[n][:], scalar1=c_cols[:, n : n + 1], scalar2=None, op0=ALU.mult
+                )
+            parked[n] = t
+
+        def finish(n, pieces):
+            width = R // pieces
+            t = stream.tile([P, R], F32, name="result", tag="result", bufs=6)
+            for r0 in range(0, R, width):
+                cols = slice(r0, r0 + width)
+                if n in parked:
+                    nc.vector.scalar_tensor_tensor(
+                        out=t[:, cols],
+                        in0=sums[n][:, cols],
+                        scalar=c_cols[:, n : n + 1],
+                        in1=parked[n][:, cols],
+                        op0=ALU.mult,
+                        op1=ALU.add,
+                    )
+                else:
+                    nc.scalar.activation(
+                        out=t[:, cols], in_=sums[n][:, cols], func=ACT.Copy, scale=c_cols[:, n : n + 1]
+                    )
+                nc.sync.dma_start(out=out[n * P : (n + 1) * P, cols], in_=t[:, cols])
+
+        low = range(N_TILES // 2)
+        high = range(N_TILES // 2, N_TILES)
+
+        for g in range(FIRST):
+            width = R // 4 if g == 0 else R // 2
+            last = None
+            for r0 in range(0, R, width):
+                piece = (g, r0, r0 + width)
+                tanh(piece)
+                scale_rows(piece)
+                if last is not None:
+                    quantize_s(last)
+                last = piece
+            quantize_s(last)
+            for n in low:
+                if g == 0:
+                    open_sum(n)
+                multiply(n, g, g == 0, g == FIRST - 1)
+
+        later = [(g, r0, r0 + R // 2) for g in range(FIRST, PASSES) for r0 in (0, R // 2)]
+        last = None
+        waiting = list(low)
+        for i, piece in enumerate(later):
+            tanh(piece)
+            scale_rows(piece)
+            if last is not None:
+                quantize_s(last)
+            last = piece
+            if i > 0:
+                for n in waiting[:2]:
+                    park(n, "scalar" if n % 2 == 0 else "vector")
+                    m = n + N_TILES // 2
+                    open_sum(m)
+                    for g in range(FIRST):
+                        multiply(m, g, g == 0, False)
+                waiting = waiting[2:]
+        for g in range(FIRST, REST):
+            for n in high:
+                multiply(n, g, False, False)
+
+        pairs = list(range(N_TILES // 2, N_TILES, PAIR)) + list(range(0, N_TILES // 2, PAIR))
+        on_scalar = list(pairs)
+        on_vector = list(pairs)
+        group_a(REST, on_vector.pop(0), "vector")
+        quantize_s(last)
+        closed = []
+        for k, n0 in enumerate(pairs):
+            while on_scalar and len(pairs) - len(on_scalar) < k + 3:
+                group_a(REST + 1, on_scalar.pop(0), "scalar")
+            while on_vector and len(pairs) - len(on_vector) < k + 2:
+                group_a(REST, on_vector.pop(0), "vector")
+            for g in range(REST, PASSES):
+                quantize_a(g, n0)
+            for n in range(n0, n0 + PAIR):
+                if n in low:
+                    open_sum(n)
+                    for g in range(FIRST, REST):
+                        multiply(n, g, g == FIRST, False)
+                for g in range(REST, PASSES):
+                    multiply(n, g, False, g == PASSES - 1)
+            for n in closed:
+                finish(n, 1)
+            closed = list(range(n0, n0 + PAIR))
+        finish(closed[0], 1)
+        finish(closed[1], 2)

@@ -51,8 +51,9 @@ def tile_hager_adjoint_step_s1_kernel(
             return t
 
         scales_lo_first = plane("scales_lo_first", FIRST)
+        scales_hi_first = plane("scales_hi_first", FIRST)
+        scales_hi_later = plane("scales_hi_later", REST - FIRST)
         scales_lo_later = plane("scales_lo_later", REST - FIRST)
-        scales_hi = plane("scales_hi", REST)
 
         nc.scalar.dma_start(out=rows[0:4, :K_PASS], in_=d_rest[0 : 4 * K_PASS].rearrange("(g k) -> g k", k=K_PASS))
         nc.scalar.dma_start(out=rows[4:6, :K_PASS], in_=d_rest[4 * K_PASS : ML].rearrange("(g k) -> g k", k=K_PASS))
@@ -107,22 +108,22 @@ def tile_hager_adjoint_step_s1_kernel(
         load_y(1, whole)
         load_words(0, 1, 0)
         load_scales(scales_lo_first, 0, FIRST, 0)
-        load_words(1, 2, 0)
-        load_y(2, whole)
-        load_words(2, FIRST, 0)
-        load_y(3, whole)
+        for g in range(1, FIRST):
+            load_y(g + 1, whole)
+            load_words(g, g + 1, 0)
+        load_y(FIRST + 1, whole)
         load_words(0, FIRST, 1)
-        load_y(4, whole)
-        load_scales(scales_hi, 0, REST, 1)
-        load_words(FIRST, REST, 1)
-        for g in range(5, PASSES):
-            load_y(g, whole)
+        load_scales(scales_hi_first, 0, FIRST, 1)
         for g in range(REST, PASSES):
-            load_a(g, 1)
+            load_y(g, whole)
+        load_words(FIRST, REST, 1)
+        load_scales(scales_hi_later, FIRST, REST, 1)
+        load_a(REST + 1, 1)
+        load_a(REST, 1)
         load_scales(scales_lo_later, FIRST, REST, 0)
         load_words(FIRST, REST, 0)
-        for g in range(REST, PASSES):
-            load_a(g, 0)
+        load_a(REST + 1, 0)
+        load_a(REST, 0)
 
         turned = banks.tile([P, PACK + 1, P], BF16, name="turned", tag="bank7")
         for j in range(PACK):
@@ -170,8 +171,8 @@ def tile_hager_adjoint_step_s1_kernel(
             t = stream.tile([P, PAIR * P, PACK], BF16, name="grouped", tag="grouped", bufs=8, align_bytes=64)
             at = n0 * P % HALF
             src = a_tiles[g, n0 * P // HALF][:, :, at : at + PAIR * P]
-            src = src.rearrange("p j n -> p n j")
-            dst = t[:]
+            src = src.rearrange("p j (n i) -> p n j i", i=4)
+            dst = t[:].rearrange("p (n i) j -> p n j i", i=4)
             if engine == "scalar":
                 nc.scalar.copy(out=dst, in_=src)
             else:

@@ -25,6 +25,7 @@ N_TILES = N // P
 HALF = N // 2
 FIRST = 4
 PAIR = 2
+RUN = 4
 
 
 def tile_hager_adjoint_step_s1_kernel(
@@ -42,11 +43,11 @@ def tile_hager_adjoint_step_s1_kernel(
         nc.gpsimd.memset(warm[:], 0.0)
         ident = keep.tile([P, P], BF16, name="ident")
         make_identity(nc, ident[:])
-        rows = keep.tile([P, K_PASS + P], BF16, name="rows", align_bytes=64)
+        rows = keep.tile([P, K_PASS + P], BF16, name="rows", align_bytes=256)
         nc.vector.memset(rows[:], 0.0)
 
         def plane(name, groups):
-            t = keep.tile([P, groups, HALF], U8, name=name, align_bytes=64)
+            t = keep.tile([P, groups, HALF], U8, name=name, align_bytes=256)
             nc.vector.memset(t[:].rearrange("p g n -> p (g n)").bitcast(I32), 0)
             return t
 
@@ -55,10 +56,8 @@ def tile_hager_adjoint_step_s1_kernel(
         scales_hi_later = plane("scales_hi_later", REST - FIRST)
         scales_lo_later = plane("scales_lo_later", REST - FIRST)
 
-        nc.scalar.dma_start(out=rows[0:4, :K_PASS], in_=d_rest[0 : 4 * K_PASS].rearrange("(g k) -> g k", k=K_PASS))
-        nc.scalar.dma_start(out=rows[4:6, :K_PASS], in_=d_rest[4 * K_PASS : ML].rearrange("(g k) -> g k", k=K_PASS))
-        nc.scalar.dma_start(out=rows[6:8, :K_PASS], in_=d_heavy.rearrange("(g k) -> g k", k=K_PASS))
-        nc.scalar.dma_start(out=rows[0:N_TILES, K_PASS:], in_=c.rearrange("(n m) -> n m", m=P))
+        d_first = keep.tile([P, PACK], BF16, name="d_first")
+        nc.scalar.dma_start(out=d_first[:], in_=d_rest[0:K_PASS].rearrange("(p j) -> p j", j=PACK))
         nc.scalar.activation(out=warm[:], in_=warm[:], func=ACT.Tanh)
 
         y_tiles = {}
@@ -75,7 +74,7 @@ def tile_hager_adjoint_step_s1_kernel(
         words = {}
 
         def load_words(g0, g1, half):
-            t = keep.tile([P, g1 - g0, 2 * HALF], U8, name="w" + str(half) + "_" + str(g0), align_bytes=64)
+            t = keep.tile([P, g1 - g0, 2 * HALF], U8, name="w" + str(half) + "_" + str(g0), align_bytes=256)
             src = rest_words[g0:g1, :, half * 2 * HALF : (half + 1) * 2 * HALF].rearrange("g p b -> p g b")
             nc.sync.dma_start(out=t[:].bitcast(I32), in_=src.bitcast(I32))
             for g in range(g0, g1):
@@ -103,8 +102,12 @@ def tile_hager_adjoint_step_s1_kernel(
             a_tiles[g, half] = t
 
         whole = slice(0, R)
-        load_y(0, slice(0, R // 2))
-        load_y(0, slice(R // 2, R))
+        load_y(0, slice(0, P))
+        load_y(0, slice(P, R))
+        nc.sync.dma_start(out=rows[0:4, :K_PASS], in_=d_rest[0 : 4 * K_PASS].rearrange("(g k) -> g k", k=K_PASS))
+        nc.sync.dma_start(out=rows[4:6, :K_PASS], in_=d_rest[4 * K_PASS : ML].rearrange("(g k) -> g k", k=K_PASS))
+        nc.sync.dma_start(out=rows[6:8, :K_PASS], in_=d_heavy.rearrange("(g k) -> g k", k=K_PASS))
+        nc.sync.dma_start(out=rows[0:N_TILES, K_PASS:], in_=c.rearrange("(n m) -> n m", m=P))
         load_y(1, whole)
         load_words(0, 1, 0)
         load_scales(scales_lo_first, 0, FIRST, 0)
@@ -130,29 +133,30 @@ def tile_hager_adjoint_step_s1_kernel(
             nc.tensor.transpose(turned[:, j, :], rows[:, j:K_PASS:PACK], ident[:])
         nc.tensor.transpose(turned[:, PACK, :], rows[:, K_PASS:], ident[:])
         d_cols = keep.tile([P, PASSES, PACK], F32, name="d_cols")
-        nc.vector.tensor_copy(out=d_cols[:], in_=turned[:, :PACK, :PASSES].rearrange("p j g -> p g j"))
         c_cols = keep.tile([P, N_TILES], F32, name="c_cols")
-        nc.vector.tensor_copy(out=c_cols[:], in_=turned[:, PACK, :N_TILES])
 
-        s_codes = [keep.tile([P, R], U32, name="s_codes" + str(g), align_bytes=64) for g in range(PASSES)]
-        s_scales = [keep.tile([P, R], U8, name="s_scales" + str(g), align_bytes=64) for g in range(PASSES)]
+        s_codes = [keep.tile([P, R], U32, name="s_codes" + str(g), align_bytes=256) for g in range(PASSES)]
+        s_scales = [keep.tile([P, R], U8, name="s_scales" + str(g), align_bytes=256) for g in range(PASSES)]
         smooth = {}
         scaled = {}
 
         def tanh(piece):
             g, r0, r1 = piece
             y, at = y_tiles[g, r0]
-            t = stream.tile([P, r1 - r0, PACK], F32, name="smooth", tag="smooth", bufs=4)
-            nc.scalar.activation(
-                out=t[:], in_=y[:, :, at : at + r1 - r0].rearrange("p j w -> p w j"), func=ACT.Tanh
-            )
+            t = stream.tile([P, PACK, r1 - r0], F32, name="smooth", tag="smooth", bufs=4)
+            nc.scalar.activation(out=t[:], in_=y[:, :, at : at + r1 - r0], func=ACT.Tanh)
             smooth[piece] = t
 
         def scale_rows(piece):
             g, r0, r1 = piece
-            t = stream.tile([P, r1 - r0, PACK], BF16, name="scaled", tag="scaled", bufs=4, align_bytes=64)
-            d = d_cols[:, g, :].unsqueeze(1).to_broadcast([P, r1 - r0, PACK])
-            nc.vector.tensor_tensor(out=t[:], in0=smooth[piece][:], in1=d, op=ALU.mult)
+            t = stream.tile([P, r1 - r0, PACK], BF16, name="scaled", tag="scaled", bufs=4, align_bytes=256)
+            d = d_first[:] if g == 0 else d_cols[:, g, :]
+            nc.vector.tensor_tensor(
+                out=t[:].rearrange("p (w i) j -> p w j i", i=RUN),
+                in0=smooth[piece][:].rearrange("p j (w i) -> p w j i", i=RUN),
+                in1=d.unsqueeze(1).unsqueeze(3).to_broadcast([P, (r1 - r0) // RUN, PACK, RUN]),
+                op=ALU.mult,
+            )
             scaled[piece] = t
 
         def quantize_s(piece):
@@ -168,7 +172,7 @@ def tile_hager_adjoint_step_s1_kernel(
         a_scales = {}
 
         def group_a(g, n0, engine):
-            t = stream.tile([P, PAIR * P, PACK], BF16, name="grouped", tag="grouped", bufs=8, align_bytes=64)
+            t = stream.tile([P, PAIR * P, PACK], BF16, name="grouped", tag="grouped", bufs=8, align_bytes=256)
             at = n0 * P % HALF
             src = a_tiles[g, n0 * P // HALF][:, :, at : at + PAIR * P]
             src = src.rearrange("p j (n i) -> p n j i", i=4)
@@ -180,8 +184,8 @@ def tile_hager_adjoint_step_s1_kernel(
             grouped[g, n0] = t
 
         def quantize_a(g, n0):
-            codes = keep.tile([P, PAIR * P], U32, name="a_codes" + str(g) + "_" + str(n0), align_bytes=64)
-            scales = keep.tile([P, PAIR * P], U8, name="a_scales" + str(g) + "_" + str(n0), align_bytes=64)
+            codes = keep.tile([P, PAIR * P], U32, name="a_codes" + str(g) + "_" + str(n0), align_bytes=256)
+            scales = keep.tile([P, PAIR * P], U8, name="a_scales" + str(g) + "_" + str(n0), align_bytes=256)
             nc.vector.quantize_mx(
                 out=codes[:].bitcast(FP8X4), scales=scales[:], in_=grouped[g, n0][:].rearrange("p n j -> p (n j)")
             )
@@ -214,14 +218,9 @@ def tile_hager_adjoint_step_s1_kernel(
 
         parked = {}
 
-        def park(n, engine):
+        def park(n):
             t = keep.tile([P, R], F32, name="parked" + str(n))
-            if engine == "scalar":
-                nc.scalar.activation(out=t[:], in_=sums[n][:], func=ACT.Copy, scale=c_cols[:, n : n + 1])
-            else:
-                nc.vector.tensor_scalar(
-                    out=t[:], in0=sums[n][:], scalar1=c_cols[:, n : n + 1], scalar2=None, op0=ALU.mult
-                )
+            nc.scalar.activation(out=t[:], in_=sums[n][:], func=ACT.Copy, scale=c_cols[:, n : n + 1])
             parked[n] = t
 
         def finish(n, pieces):
@@ -258,6 +257,9 @@ def tile_hager_adjoint_step_s1_kernel(
                     quantize_s(last)
                 last = piece
             quantize_s(last)
+            if g == 0:
+                nc.vector.tensor_copy(out=d_cols[:], in_=turned[:, :PACK, :PASSES].rearrange("p j g -> p g j"))
+                nc.vector.tensor_copy(out=c_cols[:], in_=turned[:, PACK, :N_TILES])
             for n in low:
                 if g == 0:
                     open_sum(n)
@@ -272,9 +274,12 @@ def tile_hager_adjoint_step_s1_kernel(
             if last is not None:
                 quantize_s(last)
             last = piece
-            if i > 0:
+            if piece[2] == R:
+                quantize_s(last)
+                last = None
+            if i > 1:
                 for n in waiting[:2]:
-                    park(n, "scalar" if n % 2 == 0 else "vector")
+                    park(n)
                     m = n + N_TILES // 2
                     open_sum(m)
                     for g in range(FIRST):
@@ -287,8 +292,6 @@ def tile_hager_adjoint_step_s1_kernel(
         pairs = list(range(N_TILES // 2, N_TILES, PAIR)) + list(range(0, N_TILES // 2, PAIR))
         on_scalar = list(pairs)
         on_vector = list(pairs)
-        group_a(REST, on_vector.pop(0), "vector")
-        quantize_s(last)
         closed = []
         for k, n0 in enumerate(pairs):
             while on_scalar and len(pairs) - len(on_scalar) < k + 3:

from contextlib import ExitStack

import concourse.mybir as mybir
from concourse.masks import make_identity

F32 = mybir.dt.float32
BF16 = mybir.dt.bfloat16
I32 = mybir.dt.int32
U32 = mybir.dt.uint32
U8 = mybir.dt.uint8
FP8X4 = mybir.dt.float8_e4m3fn_x4
FP4X4 = mybir.dt.float4_e2m1fn_x4
ACT = mybir.ActivationFunctionType
ALU = mybir.AluOpType

MH, ML, N, R = 1024, 3072, 2048, 512
FLOPS = 2 * (MH + ML) * N * R

P = 128
PACK = 4
K_PASS = P * PACK
REST = ML // K_PASS
PASSES = (MH + ML) // K_PASS
N_TILES = N // P
HALF = N // 2
FIRST = 4
PAIR = 2
RUN = 4


def tile_hager_adjoint_step_s1_kernel(
    tc, y_heavy, y_rest, d_heavy, d_rest, c, a_heavy, rest_words, rest_scales, out
):
    nc = tc.nc

    with ExitStack() as ctx:
        keep = ctx.enter_context(tc.tile_pool(name="keep", bufs=1))
        stream = ctx.enter_context(tc.tile_pool(name="stream", bufs=4))
        banks = ctx.enter_context(tc.psum_pool(name="banks", bufs=1))
        ctx.enter_context(tc.manual_schedule())

        warm = keep.tile([P, 1], F32, name="warm")
        nc.gpsimd.memset(warm[:], 0.0)
        ident = keep.tile([P, P], BF16, name="ident")
        make_identity(nc, ident[:])
        rows = keep.tile([P, K_PASS + P], BF16, name="rows", align_bytes=256)
        nc.vector.memset(rows[:], 0.0)

        def plane(name, groups):
            t = keep.tile([P, groups, HALF], U8, name=name, align_bytes=256)
            nc.vector.memset(t[:].rearrange("p g n -> p (g n)").bitcast(I32), 0)
            return t

        scales_lo_first = plane("scales_lo_first", FIRST)
        scales_hi_first = plane("scales_hi_first", FIRST)
        scales_hi_later = plane("scales_hi_later", REST - FIRST)
        scales_lo_later = plane("scales_lo_later", REST - FIRST)

        d_first = keep.tile([P, PACK], BF16, name="d_first")
        nc.scalar.dma_start(out=d_first[:], in_=d_rest[0:K_PASS].rearrange("(p j) -> p j", j=PACK))
        nc.scalar.activation(out=warm[:], in_=warm[:], func=ACT.Tanh)

        y_tiles = {}

        def load_y(g, cols):
            src = y_rest if g < REST else y_heavy
            row0 = (g if g < REST else g - REST) * K_PASS
            width = cols.stop - cols.start
            t = keep.tile([P, PACK, width], BF16, name="y" + str(g) + "_" + str(cols.start))
            nc.sync.dma_start(out=t[:], in_=src[row0 : row0 + K_PASS, cols].rearrange("(p j) w -> p j w", j=PACK))
            for q0 in range(cols.start, cols.stop, P):
                y_tiles[g, q0] = (t, q0 - cols.start)

        words = {}

        def load_words(g0, g1, half):
            t = keep.tile([P, g1 - g0, 2 * HALF], U8, name="w" + str(half) + "_" + str(g0), align_bytes=256)
            src = rest_words[g0:g1, :, half * 2 * HALF : (half + 1) * 2 * HALF].rearrange("g p b -> p g b")
            nc.sync.dma_start(out=t[:].bitcast(I32), in_=src.bitcast(I32))
            for g in range(g0, g1):
                words[g, half] = t[:, g - g0, :]

        planes = {}

        def load_scales(t, g0, g1, half):
            src = rest_scales[g0:g1, :, half * HALF : (half + 1) * HALF].rearrange("g q n -> q g n")
            for quad in range(4):
                nc.sync.dma_start(
                    out=t[32 * quad : 32 * quad + 4, :, :].bitcast(I32),
                    in_=src[4 * quad : 4 * quad + 4, :, :].bitcast(I32),
                )
            for g in range(g0, g1):
                planes[g, half] = t[:, g - g0, :]

        a_tiles = {}

        def load_a(g, half):
            row0 = (g - REST) * K_PASS
            t = keep.tile([P, PACK, HALF], BF16, name="a" + str(g) + "_" + str(half))
            src = a_heavy[row0 : row0 + K_PASS, half * HALF : (half + 1) * HALF]
            nc.sync.dma_start(out=t[:], in_=src.rearrange("(p j) n -> p j n", j=PACK))
            a_tiles[g, half] = t

        whole = slice(0, R)
        load_y(0, slice(0, P))
        load_y(0, slice(P, R))
        nc.sync.dma_start(out=rows[0:4, :K_PASS], in_=d_rest[0 : 4 * K_PASS].rearrange("(g k) -> g k", k=K_PASS))
        nc.sync.dma_start(out=rows[4:6, :K_PASS], in_=d_rest[4 * K_PASS : ML].rearrange("(g k) -> g k", k=K_PASS))
        nc.sync.dma_start(out=rows[6:8, :K_PASS], in_=d_heavy.rearrange("(g k) -> g k", k=K_PASS))
        nc.sync.dma_start(out=rows[0:N_TILES, K_PASS:], in_=c.rearrange("(n m) -> n m", m=P))
        load_y(1, whole)
        load_words(0, 1, 0)
        load_scales(scales_lo_first, 0, FIRST, 0)
        for g in range(1, FIRST):
            load_y(g + 1, whole)
            load_words(g, g + 1, 0)
        load_y(FIRST + 1, whole)
        load_words(0, FIRST, 1)
        load_scales(scales_hi_first, 0, FIRST, 1)
        for g in range(REST, PASSES):
            load_y(g, whole)
        load_words(FIRST, REST, 1)
        load_scales(scales_hi_later, FIRST, REST, 1)
        load_a(REST + 1, 1)
        load_a(REST, 1)
        load_scales(scales_lo_later, FIRST, REST, 0)
        load_words(FIRST, REST, 0)
        load_a(REST + 1, 0)
        load_a(REST, 0)

        turned = banks.tile([P, PACK + 1, P], BF16, name="turned", tag="bank7")
        for j in range(PACK):
            nc.tensor.transpose(turned[:, j, :], rows[:, j:K_PASS:PACK], ident[:])
        nc.tensor.transpose(turned[:, PACK, :], rows[:, K_PASS:], ident[:])
        d_cols = keep.tile([P, PASSES, PACK], F32, name="d_cols")
        c_cols = keep.tile([P, N_TILES], F32, name="c_cols")

        s_codes = [keep.tile([P, R], U32, name="s_codes" + str(g), align_bytes=256) for g in range(PASSES)]
        s_scales = [keep.tile([P, R], U8, name="s_scales" + str(g), align_bytes=256) for g in range(PASSES)]
        smooth = {}
        scaled = {}

        def tanh(piece):
            g, r0, r1 = piece
            y, at = y_tiles[g, r0]
            t = stream.tile([P, PACK, r1 - r0], F32, name="smooth", tag="smooth", bufs=4)
            nc.scalar.activation(out=t[:], in_=y[:, :, at : at + r1 - r0], func=ACT.Tanh)
            smooth[piece] = t

        def scale_rows(piece):
            g, r0, r1 = piece
            t = stream.tile([P, r1 - r0, PACK], BF16, name="scaled", tag="scaled", bufs=4, align_bytes=256)
            d = d_first[:] if g == 0 else d_cols[:, g, :]
            nc.vector.tensor_tensor(
                out=t[:].rearrange("p (w i) j -> p w j i", i=RUN),
                in0=smooth[piece][:].rearrange("p j (w i) -> p w j i", i=RUN),
                in1=d.unsqueeze(1).unsqueeze(3).to_broadcast([P, (r1 - r0) // RUN, PACK, RUN]),
                op=ALU.mult,
            )
            scaled[piece] = t

        def quantize_s(piece):
            g, r0, r1 = piece
            nc.vector.quantize_mx(
                out=s_codes[g][:, r0:r1].bitcast(FP8X4),
                scales=s_scales[g][:, r0:r1],
                in_=scaled[piece][:].rearrange("p w j -> p (w j)"),
            )

        grouped = {}
        a_codes = {}
        a_scales = {}

        def group_a(g, n0, engine):
            t = stream.tile([P, PAIR * P, PACK], BF16, name="grouped", tag="grouped", bufs=8, align_bytes=256)
            at = n0 * P % HALF
            src = a_tiles[g, n0 * P // HALF][:, :, at : at + PAIR * P]
            src = src.rearrange("p j (n i) -> p n j i", i=4)
            dst = t[:].rearrange("p (n i) j -> p n j i", i=4)
            if engine == "scalar":
                nc.scalar.copy(out=dst, in_=src)
            else:
                nc.vector.tensor_copy(out=dst, in_=src)
            grouped[g, n0] = t

        def quantize_a(g, n0):
            codes = keep.tile([P, PAIR * P], U32, name="a_codes" + str(g) + "_" + str(n0), align_bytes=256)
            scales = keep.tile([P, PAIR * P], U8, name="a_scales" + str(g) + "_" + str(n0), align_bytes=256)
            nc.vector.quantize_mx(
                out=codes[:].bitcast(FP8X4), scales=scales[:], in_=grouped[g, n0][:].rearrange("p n j -> p (n j)")
            )
            for i in range(PAIR):
                a_codes[g, n0 + i] = codes[:, i * P : (i + 1) * P]
                a_scales[g, n0 + i] = scales[:, i * P : (i + 1) * P]

        sums = {}

        def open_sum(n):
            sums[n] = banks.tile([P, R], F32, name="sum" + str(n % 8), tag="bank" + str(n % 8))

        def multiply(n, g, start, stop):
            if g < REST:
                half, at = divmod(n, N_TILES // 2)
                codes = words[g, half][:, 2 * P * at : 2 * P * (at + 1)].bitcast(FP4X4)
                scales = planes[g, half][:, P * at : P * (at + 1)]
            else:
                codes = a_codes[g, n].bitcast(FP8X4)
                scales = a_scales[g, n]
            nc.tensor.matmul_mx(
                out=sums[n][:],
                lhsT=codes,
                lhsT_scale=scales,
                rhs=s_codes[g][:].bitcast(FP8X4),
                rhs_scale=s_scales[g][:],
                start=start,
                stop=stop,
            )

        parked = {}

        def park(n):
            t = keep.tile([P, R], F32, name="parked" + str(n))
            nc.scalar.activation(out=t[:], in_=sums[n][:], func=ACT.Copy, scale=c_cols[:, n : n + 1])
            parked[n] = t

        def finish(n, pieces):
            width = R // pieces
            t = stream.tile([P, R], F32, name="result", tag="result", bufs=6)
            for r0 in range(0, R, width):
                cols = slice(r0, r0 + width)
                if n in parked:
                    nc.vector.scalar_tensor_tensor(
                        out=t[:, cols],
                        in0=sums[n][:, cols],
                        scalar=c_cols[:, n : n + 1],
                        in1=parked[n][:, cols],
                        op0=ALU.mult,
                        op1=ALU.add,
                    )
                else:
                    nc.scalar.activation(
                        out=t[:, cols], in_=sums[n][:, cols], func=ACT.Copy, scale=c_cols[:, n : n + 1]
                    )
                nc.sync.dma_start(out=out[n * P : (n + 1) * P, cols], in_=t[:, cols])

        low = range(N_TILES // 2)
        high = range(N_TILES // 2, N_TILES)

        for g in range(FIRST):
            width = R // 4 if g == 0 else R // 2
            last = None
            for r0 in range(0, R, width):
                piece = (g, r0, r0 + width)
                tanh(piece)
                scale_rows(piece)
                if last is not None:
                    quantize_s(last)
                last = piece
            quantize_s(last)
            if g == 0:
                nc.vector.tensor_copy(out=d_cols[:], in_=turned[:, :PACK, :PASSES].rearrange("p j g -> p g j"))
                nc.vector.tensor_copy(out=c_cols[:], in_=turned[:, PACK, :N_TILES])
            for n in low:
                if g == 0:
                    open_sum(n)
                multiply(n, g, g == 0, g == FIRST - 1)

        later = [(g, r0, r0 + R // 2) for g in range(FIRST, PASSES) for r0 in (0, R // 2)]
        last = None
        waiting = list(low)
        for i, piece in enumerate(later):
            tanh(piece)
            scale_rows(piece)
            if last is not None:
                quantize_s(last)
            last = piece
            if piece[2] == R:
                quantize_s(last)
                last = None
            if i > 1:
                for n in waiting[:2]:
                    park(n)
                    m = n + N_TILES // 2
                    open_sum(m)
                    for g in range(FIRST):
                        multiply(m, g, g == 0, False)
                waiting = waiting[2:]
        for g in range(FIRST, REST):
            for n in high:
                multiply(n, g, False, False)

        pairs = list(range(N_TILES // 2, N_TILES, PAIR)) + list(range(0, N_TILES // 2, PAIR))
        on_scalar = list(pairs)
        on_vector = list(pairs)
        closed = []
        for k, n0 in enumerate(pairs):
            while on_scalar and len(pairs) - len(on_scalar) < k + 3:
                group_a(REST + 1, on_scalar.pop(0), "scalar")
            while on_vector and len(pairs) - len(on_vector) < k + 2:
                group_a(REST, on_vector.pop(0), "vector")
            for g in range(REST, PASSES):
                quantize_a(g, n0)
            for n in range(n0, n0 + PAIR):
                if n in low:
                    open_sum(n)
                    for g in range(FIRST, REST):
                        multiply(n, g, g == FIRST, False)
                for g in range(REST, PASSES):
                    multiply(n, g, False, g == PASSES - 1)
            for n in closed:
                finish(n, 1)
            closed = list(range(n0, n0 + PAIR))
        finish(closed[0], 1)
        finish(closed[1], 2)
